import numpy as np
import ml_dtypes


def mxq(x, axis, fmt="e4m3"):
    dtype, down = {"e4m3": (ml_dtypes.float8_e4m3fn, 7), "e5m2": (ml_dtypes.float8_e5m2, 14)}[fmt]
    v = np.moveaxis(np.asarray(x, np.float32).astype(ml_dtypes.bfloat16).astype(np.float64), axis, -1)
    blocks = v.reshape(v.shape[:-1] + (-1, 32))
    amax = np.abs(blocks).max(-1, keepdims=True)
    byte = np.maximum(np.where(amax > 0, np.frexp(amax)[1] - 1 + 127, 0) - down, 1)
    scale = np.exp2(byte - 127.0)
    codes = (blocks / scale).astype(np.float32).astype(dtype).astype(np.float64)
    return np.moveaxis((codes * scale).reshape(v.shape), -1, axis)


WIDE = False


def mx_kscale(k):
    if not WIDE:
        return np.ones(k)
    levels = np.array([10, -10, 5, -5, 0])
    if k % 512:
        return np.exp2(np.random.permutation(np.resize(levels, k // 32))).repeat(32)
    a = np.empty((k // 512, 16))
    for p in range(k // 512):
        a[p, :8] = np.random.permutation(np.resize(levels, 8))
        for g in range(8):
            far = levels[np.abs(levels - a[p, g]) >= 10]
            a[p, g + 8] = far[np.random.randint(len(far))]
    return np.exp2(a.ravel()).repeat(32)


def f64(x):
    return np.asarray(x).astype(np.float64)


def striped(idx):
    return np.tile(idx.reshape(-1, 16).T, (8, 1)).astype(np.uint16)


def unstriped(offs):
    return offs[:16].T.reshape(-1).astype(np.int64)


def gelu(v):
    return 0.5 * v * (1.0 + np.tanh(np.sqrt(2.0 / np.pi) * (v + 0.044715 * v**3)))


K, T, E, C, N = 1536, 512, 4, 256, 256


def by_expert(wq, xq):
    return np.concatenate([wq[e].T @ xq[:, e * C:(e + 1) * C] for e in range(E)], axis=1)


def setup_inputs():
    n = np.random.standard_normal
    s = mx_kscale(K)[:, None]
    first = np.random.permutation(np.repeat(np.arange(E), T // E))
    second = (first + 1 + np.random.permutation(np.repeat(np.arange(E - 1), -(-T // (E - 1)))[:T])) % E
    while np.bincount(second, minlength=E).max() != T // E:
        load = np.bincount(second, minlength=E); hi, lo = int(load.argmax()), int(load.argmin())
        t = np.flatnonzero((second == hi) & (first != lo))[0]; second[t] = lo
    slot_token = np.empty(E * C, np.int64); pos = np.empty((2, T), np.int64); fill = np.zeros(E, np.int64)
    place = np.stack([np.random.permutation(C) for _ in range(E)])
    for r, deal in enumerate((first, second)):
        for t in np.random.permutation(T):
            e = deal[t]; j = e * C + place[e, fill[e]]; fill[e] += 1; slot_token[j] = t; pos[r, t] = j
    g = np.random.uniform(0.2, 0.8, T)
    return {
        "xT": (n((K, T)) * s).astype(np.float32),
        "w": (n((E + 1, K, N)) / np.sqrt(K) / s[None]).astype(np.float32),
        "b": (0.3 * n((N, E + 1))).astype(np.float32),
        "gate": np.stack([np.tile(g, (N, 1)), np.tile(1.0 - g, (N, 1))]).astype(np.float32),
        "offs": striped(slot_token),
        "pos1": striped(pos[0]),
        "pos2": striped(pos[1]),
    }


def reference(xT, w, b, gate, offs, pos1, pos2):
    idx = unstriped(offs)
    wq = mxq(f64(w), 1, "e4m3")
    xs = mxq(f64(xT), 0, "e4m3")
    ys = gelu((wq[E].T @ xs) + f64(b)[:, E:])
    xq = mxq(f64(xT)[:, idx], 0, "e4m3")
    y = by_expert(wq, xq)
    y = gelu(y + np.repeat(f64(b)[:, :E], C, axis=1))
    return ys + f64(gate[0]) * y[:, unstriped(pos1)] + f64(gate[1]) * y[:, unstriped(pos2)]

@@ -1,0 +1,271 @@
+from contextlib import ExitStack
+
+import concourse.mybir as mybir
+
+F32 = mybir.dt.float32
+BF16 = mybir.dt.bfloat16
+I32 = mybir.dt.int32
+U32 = mybir.dt.uint32
+U16 = mybir.dt.uint16
+U8 = mybir.dt.uint8
+FP8X4 = mybir.dt.float8_e4m3fn_x4
+ADD = mybir.AluOpType.add
+MULT = mybir.AluOpType.mult
+GELU = mybir.ActivationFunctionType.Gelu_apprx_tanh
+
+P = 128
+K, T, E, C, N = 1536, 512, 4, 256, 256
+S = E * C
+G = K // 512
+M = N // P
+FLOPS = 2 * K * N * (S + T)
+
+GPS = ((0, 0), (0, 1), (1, 0), (1, 2))
+
+
+def tile_moe_shr_lin_gelu_kernel(tc, xT, w, b, gate, offs, pos1, pos2, out):
+    nc = tc.nc
+    planes = 2 * G
+    with ExitStack() as ctx:
+        keep = ctx.enter_context(tc.tile_pool(name="keep", bufs=1))
+        ring = ctx.enter_context(tc.tile_pool(name="ring", bufs=2))
+        psum = ctx.enter_context(tc.psum_pool(name="psum", bufs=8))
+
+        offs_t = keep.tile([P, S // 16], U16, name="offs_t")
+        pos1_t = keep.tile([P, T // 16], U16, name="pos1_t")
+        pos2_t = keep.tile([P, T // 16], U16, name="pos2_t")
+        bias = keep.tile([P, M, E + 1], F32, name="bias")
+        gates = keep.tile([P, 2, M, T], F32, name="gates")
+        xp = keep.tile([P, planes * T * 2], BF16, name="xp", align_bytes=64)
+        y = [keep.tile([P, S], F32, name=f"y{m}") for m in range(M)]
+        ys = [keep.tile([P, T], F32, name=f"ys{m}") for m in range(M)]
+
+        nc.scalar.dma_start(out=bias[:], in_=b.rearrange("(m p) e -> p m e", p=P))
+        warm = keep.tile([P, 1], F32, name="warm")
+        nc.vector.memset(warm[:], 0.0)
+        warm2 = keep.tile([P, 1], F32, name="warm2")
+        nc.scalar.activation(out=warm2[:], in_=warm[:], func=GELU)
+
+        nc.sync.dma_start(offs_t[:], offs)
+        xraw, wraw = {}, {}
+
+        def load_x(q):
+            g, u = q // 2, 1 - q % 2
+            xraw[q] = keep.tile([P, 2, T], F32, name=f"xraw{q}")
+            rows = xT[g * 512 : (g + 1) * 512, :].rearrange("(p u e) t -> u p e t", u=2, e=2)
+            if q == 0:
+                for t0 in (0, T // 2):
+                    nc.sync.dma_start(out=xraw[q][:, :, t0 : t0 + T // 2], in_=rows[u][:, :, t0 : t0 + T // 2])
+            else:
+                nc.sync.dma_start(out=xraw[q][:], in_=rows[u])
+
+        def load_w(g, e):
+            wraw[g, e] = ring.tile([P, 4, N], F32, name="wraw", bufs=10)
+            nc.sync.dma_start(out=wraw[g, e][:], in_=w[e, g * 512 : (g + 1) * 512, :].rearrange("(p j) n -> p j n", j=4))
+
+        def cast_x(q, engine, t0=0, t1=T):
+            base = (planes - 1 - q) * T * 2
+            dst = xp[:, base + 2 * t0 : base + 2 * t1].rearrange("p (t e) -> p t e", e=2)
+            src = xraw[q][:, :, t0:t1].rearrange("p e t -> p t e")
+            if engine == "v":
+                nc.vector.tensor_copy(dst, src)
+            else:
+                nc.scalar.copy(dst, src)
+
+        wb = {}
+
+        def cast_w(g, e):
+            h, i = e // 2, e % 2
+            if i == 0:
+                wb[g, h] = ring.tile([P, 2, N * 4], BF16, name="wb", bufs=4, align_bytes=64)
+            dst = wb[g, h][:, i, :].rearrange("p (c i j) -> p c j i", i=4, j=4)
+            srcv = wraw[g, e][:].rearrange("p j (c i) -> p c j i", i=4)
+            if (g, e) in GPS:
+                nc.gpsimd.tensor_scalar(dst, srcv, 1.0, 0.0, MULT, ADD)
+            else:
+                nc.scalar.copy(dst, srcv)
+
+        wq, wsc = {}, {}
+
+        def quant_w(g, h):
+            n = 2 * N if h < 2 else N
+            wq[g, h] = keep.tile([P, n], U32, name=f"wq{g}{h}", align_bytes=64)
+            wsc[g, h] = keep.tile([P, n], U8, name=f"wsc{g}{h}", align_bytes=64)
+            nc.vector.quantize_mx(out=wq[g, h][:].bitcast(FP8X4), scales=wsc[g, h][:], in_=wb[g, h][:].rearrange("p i n -> p (i n)")[:, 0 : 4 * n])
+
+        gw = {}
+
+        def gather(q, cuts):
+            g, u = q // 2, 1 - q % 2
+            if u == 1:
+                gw[g] = ring.tile([P, 2, 2 * S], BF16, name="gw", align_bytes=64)
+            lo = (planes - 1 - q) * T * 2
+            hi = min(planes * T * 2, lo + 3 * T * 2)
+            s0 = 0
+            for n in cuts:
+                nc.vector.tensor_copy(
+                    gw[g][:, u, 2 * s0 : 2 * (s0 + n)].bitcast(U32),
+                    xp[:, lo:hi].bitcast(U32).indirect(offs_t[:, s0 // 16 : (s0 + n) // 16]),
+                )
+                s0 += n
+
+        xi, xq, xsc = {}, {}, {}
+
+        def weave(g, s0, s1):
+            if s0 == 0:
+                xi[g] = ring.tile([P, 4 * S], BF16, name="xi", align_bytes=64)
+            dst = xi[g][:, 4 * s0 : 4 * s1].bitcast(I32).rearrange("p (s u) -> p s u", u=2)
+            src = gw[g][:, :, 2 * s0 : 2 * s1].bitcast(I32).rearrange("p u s -> p s u")
+            nc.vector.tensor_copy(dst, src)
+
+        def quant_x(g, s0, s1):
+            if s0 == 0:
+                xq[g] = keep.tile([P, S], U32, name=f"xq{g}", align_bytes=64)
+                xsc[g] = keep.tile([P, S], U8, name=f"xsc{g}", align_bytes=64)
+            nc.vector.quantize_mx(out=xq[g][:, s0:s1].bitcast(FP8X4), scales=xsc[g][:, s0:s1], in_=xi[g][:, 4 * s0 : 4 * s1])
+
+        ti, tq, tsc = {}, {}, {}
+
+        def weave_t(g):
+            ti[g] = ring.tile([P, 4 * T], BF16, name="ti", bufs=3, align_bytes=64)
+            base = (planes - 2 - 2 * g) * T * 2
+            two = xp[:, base : base + 4 * T].bitcast(I32).rearrange("p (u t) -> p t u", u=2)
+            dst = ti[g][:].bitcast(I32).rearrange("p (t u) -> p t u", u=2)
+            nc.vector.tensor_copy(dst, two)
+
+        def quant_t(g):
+            tq[g] = keep.tile([P, T], U32, name=f"tq{g}", align_bytes=64)
+            tsc[g] = keep.tile([P, T], U8, name=f"tsc{g}", align_bytes=64)
+            nc.vector.quantize_mx(out=tq[g][:].bitcast(FP8X4), scales=tsc[g][:], in_=ti[g][:])
+
+        ps = {}
+
+        def mm(g, e, m):
+            if g == 0:
+                ps[e, m] = psum.tile([P, T], F32, name="ps")
+            h, i = e // 2, e % 2
+            n0 = i * N + m * P
+            if e < E:
+                o, r, rs = ps[e, m][:, 0:C], xq[g][:, e * C : (e + 1) * C], xsc[g][:, e * C : (e + 1) * C]
+            else:
+                o, r, rs = ps[e, m][:], tq[g][:], tsc[g][:]
+            nc.tensor.matmul_mx(
+                out=o,
+                lhsT=wq[g, h][:, n0 : n0 + P].bitcast(FP8X4),
+                lhsT_scale=wsc[g, h][:, n0 : n0 + P],
+                rhs=r.bitcast(FP8X4),
+                rhs_scale=rs,
+                start=(g == 0),
+                stop=(g == G - 1),
+            )
+
+        def gelu(e, m):
+            if e < E:
+                nc.scalar.activation(out=y[m][:, e * C : (e + 1) * C], in_=ps[e, m][:, 0:C], func=GELU, bias=bias[:, m, e : e + 1])
+            else:
+                nc.scalar.activation(out=ys[m][:], in_=ps[e, m][:], func=GELU, bias=bias[:, m, e : e + 1])
+
+        load_x(0)
+        load_x(1)
+        load_w(0, 0)
+        load_w(0, 1)
+        load_x(2)
+        load_w(0, 2)
+        load_w(0, 3)
+        load_x(3)
+        load_w(1, 0)
+        load_w(1, 1)
+        load_x(4)
+        load_w(1, 2)
+        load_w(1, 3)
+        load_x(5)
+
+        cast_x(0, "s", 0, T // 2)
+        cast_x(0, "v", T // 2, T)
+        cast_x(1, "s")
+        gather(0, (384, 384, 256))
+        gather(1, (512, 512))
+        cast_w(0, 0)
+        cast_w(0, 1)
+        cast_x(2, "s")
+        weave(0, 0, S)
+        gather(2, (1024,))
+        cast_w(0, 2)
+        cast_w(0, 3)
+        cast_x(3, "s")
+        quant_x(0, 0, S)
+        quant_w(0, 0)
+        gather(3, (1024,))
+        quant_w(0, 1)
+        for e in range(E):
+            for m in range(M):
+                mm(0, e, m)
+        cast_w(1, 0)
+        cast_w(1, 1)
+        cast_x(4, "s")
+        weave(1, 0, S)
+        gather(4, (1024,))
+        for e in range(E):
+            load_w(2, e)
+        load_w(0, E)
+        load_w(1, E)
+        nc.sync.dma_start(pos1_t[:], pos1)
+        nc.sync.dma_start(pos2_t[:], pos2)
+        nc.sync.dma_start(out=gates[:], in_=gate.rearrange("r (m p) t -> p r m t", p=P))
+        load_w(2, E)
+        cast_w(1, 2)
+        cast_w(1, 3)
+        cast_x(5, "s")
+        quant_x(1, 0, S)
+        quant_w(1, 0)
+        gather(5, (512, 512))
+        quant_w(1, 1)
+        for e in range(E):
+            for m in range(M):
+                mm(1, e, m)
+        weave(2, 0, S // 2)
+        weave(2, S // 2, S)
+        for e in range(E):
+            cast_w(2, e)
+        quant_x(2, 0, S // 2)
+        quant_x(2, S // 2, S)
+        quant_w(2, 0)
+        quant_w(2, 1)
+        for m in range(M):
+            for e in range(E):
+                mm(2, e, m)
+        for m in range(M):
+            for e in range(E):
+                gelu(e, m)
+        for g in range(G):
+            weave_t(g)
+        for g in range(G):
+            cast_w(g, E)
+        for g in range(G):
+            quant_t(g)
+        for g in range(G):
+            quant_w(g, 2)
+        for g in range(G):
+            for m in range(M):
+                mm(g, E, m)
+        for m in range(M):
+            gelu(E, m)
+
+        a = [keep.tile([P, T], F32, name=f"a{m}") for m in range(M)]
+        bb = [keep.tile([P, T], F32, name=f"bb{m}") for m in range(M)]
+        s = [keep.tile([P, T], F32, name=f"s{m}") for m in range(M)]
+        o = [keep.tile([P, T], F32, name=f"o{m}") for m in range(M)]
+
+        def pick(m, r, dst, pos):
+            nc.vector.tensor_tensor(dst[:], y[m][:].indirect(pos[:]), gates[:, r, m, :], MULT)
+
+        pick(0, 0, a[0], pos1_t)
+        pick(0, 1, bb[0], pos2_t)
+        pick(1, 0, a[1], pos1_t)
+        nc.vector.tensor_tensor(s[0][:], a[0][:], bb[0][:], ADD)
+        pick(1, 1, bb[1], pos2_t)
+        nc.vector.tensor_tensor(o[0][:], s[0][:], ys[0][:], ADD)
+        nc.sync.dma_start(out=out[0:P, :], in_=o[0][:])
+        nc.vector.tensor_tensor(s[1][:], a[1][:], bb[1][:], ADD)
+        nc.vector.tensor_tensor(o[1][:], s[1][:], ys[1][:], ADD)
+        nc.sync.dma_start(out=out[P : 2 * P, :], in_=o[1][:])

@@ -20,7 +20,9 @@ G = K // 512
 M = N // P
 FLOPS = 2 * K * N * (S + T)
 
-GPS = ((0, 0), (0, 1), (1, 0), (1, 2))
+GPS = ((0, 0), (0, 2), (1, 0), (2, 0))
+WEAVE_V = ((2, 0), (2, 512))
+WEAVE_T = (1, 2)
 
 
 def tile_moe_shr_lin_gelu_kernel(tc, xT, w, b, gate, offs, pos1, pos2, out):
@@ -114,9 +116,13 @@ def tile_moe_shr_lin_gelu_kernel(tc, xT, w, b, gate, offs, pos1, pos2, out):
         def weave(g, s0, s1):
             if s0 == 0:
                 xi[g] = ring.tile([P, 4 * S], BF16, name="xi", align_bytes=64)
-            dst = xi[g][:, 4 * s0 : 4 * s1].bitcast(I32).rearrange("p (s u) -> p s u", u=2)
-            src = gw[g][:, :, 2 * s0 : 2 * s1].bitcast(I32).rearrange("p u s -> p s u")
-            nc.vector.tensor_copy(dst, src)
+            word = I32 if (g, s0) in WEAVE_V else F32
+            dst = xi[g][:, 4 * s0 : 4 * s1].bitcast(word).rearrange("p (s u) -> p s u", u=2)
+            src = gw[g][:, :, 2 * s0 : 2 * s1].bitcast(word).rearrange("p u s -> p s u")
+            if (g, s0) in WEAVE_V:
+                nc.vector.tensor_copy(dst, src)
+            else:
+                nc.scalar.copy(dst, src)
 
         def quant_x(g, s0, s1):
             if s0 == 0:
@@ -129,9 +135,13 @@ def tile_moe_shr_lin_gelu_kernel(tc, xT, w, b, gate, offs, pos1, pos2, out):
         def weave_t(g):
             ti[g] = ring.tile([P, 4 * T], BF16, name="ti", bufs=3, align_bytes=64)
             base = (planes - 2 - 2 * g) * T * 2
-            two = xp[:, base : base + 4 * T].bitcast(I32).rearrange("p (u t) -> p t u", u=2)
-            dst = ti[g][:].bitcast(I32).rearrange("p (t u) -> p t u", u=2)
-            nc.vector.tensor_copy(dst, two)
+            word = I32 if g in WEAVE_T else F32
+            two = xp[:, base : base + 4 * T].bitcast(word).rearrange("p (u t) -> p t u", u=2)
+            dst = ti[g][:].bitcast(word).rearrange("p (t u) -> p t u", u=2)
+            if g in WEAVE_T:
+                nc.vector.tensor_copy(dst, two)
+            else:
+                nc.scalar.copy(dst, two)
 
         def quant_t(g):
             tq[g] = keep.tile([P, T], U32, name=f"tq{g}", align_bytes=64)
@@ -165,92 +175,6 @@ def tile_moe_shr_lin_gelu_kernel(tc, xT, w, b, gate, offs, pos1, pos2, out):
             else:
                 nc.scalar.activation(out=ys[m][:], in_=ps[e, m][:], func=GELU, bias=bias[:, m, e : e + 1])
 
-        load_x(0)
-        load_x(1)
-        load_w(0, 0)
-        load_w(0, 1)
-        load_x(2)
-        load_w(0, 2)
-        load_w(0, 3)
-        load_x(3)
-        load_w(1, 0)
-        load_w(1, 1)
-        load_x(4)
-        load_w(1, 2)
-        load_w(1, 3)
-        load_x(5)
-
-        cast_x(0, "s", 0, T // 2)
-        cast_x(0, "v", T // 2, T)
-        cast_x(1, "s")
-        gather(0, (384, 384, 256))
-        gather(1, (512, 512))
-        cast_w(0, 0)
-        cast_w(0, 1)
-        cast_x(2, "s")
-        weave(0, 0, S)
-        gather(2, (1024,))
-        cast_w(0, 2)
-        cast_w(0, 3)
-        cast_x(3, "s")
-        quant_x(0, 0, S)
-        quant_w(0, 0)
-        gather(3, (1024,))
-        quant_w(0, 1)
-        for e in range(E):
-            for m in range(M):
-                mm(0, e, m)
-        cast_w(1, 0)
-        cast_w(1, 1)
-        cast_x(4, "s")
-        weave(1, 0, S)
-        gather(4, (1024,))
-        for e in range(E):
-            load_w(2, e)
-        load_w(0, E)
-        load_w(1, E)
-        nc.sync.dma_start(pos1_t[:], pos1)
-        nc.sync.dma_start(pos2_t[:], pos2)
-        nc.sync.dma_start(out=gates[:], in_=gate.rearrange("r (m p) t -> p r m t", p=P))
-        load_w(2, E)
-        cast_w(1, 2)
-        cast_w(1, 3)
-        cast_x(5, "s")
-        quant_x(1, 0, S)
-        quant_w(1, 0)
-        gather(5, (512, 512))
-        quant_w(1, 1)
-        for e in range(E):
-            for m in range(M):
-                mm(1, e, m)
-        weave(2, 0, S // 2)
-        weave(2, S // 2, S)
-        for e in range(E):
-            cast_w(2, e)
-        quant_x(2, 0, S // 2)
-        quant_x(2, S // 2, S)
-        quant_w(2, 0)
-        quant_w(2, 1)
-        for m in range(M):
-            for e in range(E):
-                mm(2, e, m)
-        for m in range(M):
-            for e in range(E):
-                gelu(e, m)
-        for g in range(G):
-            weave_t(g)
-        for g in range(G):
-            cast_w(g, E)
-        for g in range(G):
-            quant_t(g)
-        for g in range(G):
-            quant_w(g, 2)
-        for g in range(G):
-            for m in range(M):
-                mm(g, E, m)
-        for m in range(M):
-            gelu(E, m)
-
         a = [keep.tile([P, T], F32, name=f"a{m}") for m in range(M)]
         bb = [keep.tile([P, T], F32, name=f"bb{m}") for m in range(M)]
         s = [keep.tile([P, T], F32, name=f"s{m}") for m in range(M)]
@@ -259,13 +183,143 @@ def tile_moe_shr_lin_gelu_kernel(tc, xT, w, b, gate, offs, pos1, pos2, out):
         def pick(m, r, dst, pos):
             nc.vector.tensor_tensor(dst[:], y[m][:].indirect(pos[:]), gates[:, r, m, :], MULT)
 
-        pick(0, 0, a[0], pos1_t)
-        pick(0, 1, bb[0], pos2_t)
-        pick(1, 0, a[1], pos1_t)
-        nc.vector.tensor_tensor(s[0][:], a[0][:], bb[0][:], ADD)
-        pick(1, 1, bb[1], pos2_t)
-        nc.vector.tensor_tensor(o[0][:], s[0][:], ys[0][:], ADD)
-        nc.sync.dma_start(out=out[0:P, :], in_=o[0][:])
-        nc.vector.tensor_tensor(s[1][:], a[1][:], bb[1][:], ADD)
-        nc.vector.tensor_tensor(o[1][:], s[1][:], ys[1][:], ADD)
-        nc.sync.dma_start(out=out[P : 2 * P, :], in_=o[1][:])
+        def load_gates():
+            nc.sync.dma_start(pos1_t[:], pos1)
+            nc.sync.dma_start(pos2_t[:], pos2)
+            nc.sync.dma_start(out=gates[:], in_=gate.rearrange("r (m p) t -> p r m t", p=P))
+
+        def pk(m, r):
+            pick(m, r, (a, bb)[r][m], (pos1_t, pos2_t)[r])
+
+        def ad(m):
+            nc.vector.tensor_tensor(s[m][:], a[m][:], bb[m][:], ADD)
+
+        def ao(m):
+            nc.vector.tensor_tensor(o[m][:], s[m][:], ys[m][:], ADD)
+
+        def st(m):
+            nc.sync.dma_start(out=out[m * P : (m + 1) * P, :], in_=o[m][:])
+
+        load_x(0)
+        load_x(1)
+        load_w(0, 0)
+        load_x(2)
+        load_w(0, 1)
+        load_x(3)
+        load_w(0, 2)
+        load_x(4)
+        load_w(0, 3)
+        load_x(5)
+        load_w(1, 0)
+        load_w(1, 1)
+        load_w(1, 2)
+        load_w(1, 3)
+        load_w(2, 0)
+        load_w(2, 1)
+        load_w(2, 2)
+        load_w(2, 3)
+        load_w(0, 4)
+        load_w(1, 4)
+        load_gates()
+        load_w(2, 4)
+        cast_x(0, "s", 0, T // 2)
+        cast_x(0, "v", T // 2, T)
+        cast_x(1, "s")
+        gather(0, (384, 384, 256,))
+        gather(1, (512, 512,))
+        cast_w(0, 0)
+        weave_t(0)
+        cast_x(2, "s")
+        cast_w(0, 1)
+        cast_x(3, "s")
+        gather(2, (1024,))
+        weave(0, 0, 1024)
+        gather(3, (1024,))
+        cast_w(0, 2)
+        cast_x(4, "s")
+        quant_x(0, 0, 1024)
+        gather(4, (1024,))
+        cast_w(0, 3)
+        cast_x(5, "s")
+        quant_t(0)
+        quant_w(0, 0)
+        weave(1, 0, 1024)
+        gather(5, (512, 512,))
+        quant_w(0, 1)
+        mm(0, 0, 0)
+        mm(0, 0, 1)
+        mm(0, 1, 0)
+        mm(0, 1, 1)
+        mm(0, 2, 0)
+        mm(0, 2, 1)
+        mm(0, 3, 0)
+        mm(0, 3, 1)
+        cast_w(1, 0)
+        cast_w(1, 1)
+        weave(2, 0, 512)
+        weave(2, 512, 1024)
+        cast_w(1, 2)
+        cast_w(1, 3)
+        quant_x(1, 0, 1024)
+        quant_w(1, 0)
+        quant_x(2, 0, 512)
+        quant_x(2, 512, 1024)
+        quant_w(1, 1)
+        mm(1, 0, 0)
+        mm(1, 0, 1)
+        mm(1, 1, 0)
+        mm(1, 1, 1)
+        mm(1, 2, 0)
+        mm(1, 2, 1)
+        mm(1, 3, 0)
+        mm(1, 3, 1)
+        cast_w(2, 0)
+        cast_w(2, 1)
+        quant_w(2, 0)
+        cast_w(2, 2)
+        cast_w(2, 3)
+        quant_w(2, 1)
+        mm(2, 0, 0)
+        mm(2, 1, 0)
+        mm(2, 2, 0)
+        mm(2, 3, 0)
+        mm(2, 0, 1)
+        mm(2, 1, 1)
+        mm(2, 2, 1)
+        mm(2, 3, 1)
+        weave_t(1)
+        quant_t(1)
+        cast_w(0, 4)
+        gelu(0, 0)
+        gelu(1, 0)
+        gelu(2, 0)
+        gelu(3, 0)
+        gelu(0, 1)
+        gelu(1, 1)
+        gelu(2, 1)
+        gelu(3, 1)
+        weave_t(2)
+        quant_t(2)
+        quant_w(0, 2)
+        cast_w(1, 4)
+        quant_w(1, 2)
+        cast_w(2, 4)
+        pk(0, 0)
+        pk(0, 1)
+        quant_w(2, 2)
+        mm(0, 4, 0)
+        mm(0, 4, 1)
+        mm(1, 4, 0)
+        mm(1, 4, 1)
+        mm(2, 4, 0)
+        mm(2, 4, 1)
+        gelu(4, 0)
+        gelu(4, 1)
+        pk(1, 0)
+        ad(0)
+        pk(1, 1)
+        ao(0)
+        st(0)
+        ad(1)
+        ao(1)
+        st(1)

@@ -20,9 +20,10 @@ G = K // 512
 M = N // P
 FLOPS = 2 * K * N * (S + T)
 
-GPS = ((0, 0), (0, 2), (1, 0), (2, 0))
-WEAVE_V = ((2, 0), (2, 512))
-WEAVE_T = (1, 2)
+GPS = ()
+WEAVE_V = ((0, 0), (1, 0), (2, 0), (2, 512), )
+WEAVE_T = (1, )
+QSG = {0: (0, 1), 1: (0, 1), 2: (2,)}
 
 
 def tile_moe_shr_lin_gelu_kernel(tc, xT, w, b, gate, offs, pos1, pos2, out):
@@ -62,7 +63,7 @@ def tile_moe_shr_lin_gelu_kernel(tc, xT, w, b, gate, offs, pos1, pos2, out):
                 nc.sync.dma_start(out=xraw[q][:], in_=rows[u])
 
         def load_w(g, e):
-            wraw[g, e] = ring.tile([P, 4, N], F32, name="wraw", bufs=10)
+            wraw[g, e] = ring.tile([P, 4, N], F32, name="wraw", bufs=8)
             nc.sync.dma_start(out=wraw[g, e][:], in_=w[e, g * 512 : (g + 1) * 512, :].rearrange("(p j) n -> p j n", j=4))
 
         def cast_x(q, engine, t0=0, t1=T):
@@ -78,8 +79,13 @@ def tile_moe_shr_lin_gelu_kernel(tc, xT, w, b, gate, offs, pos1, pos2, out):
 
         def cast_w(g, e):
             h, i = e // 2, e % 2
-            if i == 0:
-                wb[g, h] = ring.tile([P, 2, N * 4], BF16, name="wb", bufs=4, align_bytes=64)
+            if e == E:
+                if (E, QSG[g]) not in wb:
+                    wb[E, QSG[g]] = keep.tile([P, 2, N * 4], BF16, name=f"wbs{g}", align_bytes=64)
+                wb[g, h] = wb[E, QSG[g]]
+                i = QSG[g].index(g)
+            elif (g, h) not in wb:
+                wb[g, h] = ring.tile([P, 2, N * 4], BF16, name="wb", bufs=6, align_bytes=64)
             dst = wb[g, h][:, i, :].rearrange("p (c i j) -> p c j i", i=4, j=4)
             srcv = wraw[g, e][:].rearrange("p j (c i) -> p c j i", i=4)
             if (g, e) in GPS:
@@ -95,12 +101,21 @@ def tile_moe_shr_lin_gelu_kernel(tc, xT, w, b, gate, offs, pos1, pos2, out):
             wsc[g, h] = keep.tile([P, n], U8, name=f"wsc{g}{h}", align_bytes=64)
             nc.vector.quantize_mx(out=wq[g, h][:].bitcast(FP8X4), scales=wsc[g, h][:], in_=wb[g, h][:].rearrange("p i n -> p (i n)")[:, 0 : 4 * n])
 
+        def quant_s(gs):
+            n = len(gs) * N
+            codes = keep.tile([P, n], U32, name=f"wqs{gs[0]}", align_bytes=64)
+            scales = keep.tile([P, n], U8, name=f"wscs{gs[0]}", align_bytes=64)
+            nc.vector.quantize_mx(out=codes[:].bitcast(FP8X4), scales=scales[:], in_=wb[E, gs][:].rearrange("p i n -> p (i n)")[:, 0 : 4 * n])
+            for i, g in enumerate(gs):
+                wq[g, 2] = codes
+                wsc[g, 2] = scales
+
         gw = {}
 
         def gather(q, cuts):
             g, u = q // 2, 1 - q % 2
-            if u == 1:
-                gw[g] = ring.tile([P, 2, 2 * S], BF16, name="gw", align_bytes=64)
+            if g not in gw:
+                gw[g] = ring.tile([P, 2, 2 * S], BF16, name="gw", bufs=3, align_bytes=64)
             lo = (planes - 1 - q) * T * 2
             hi = min(planes * T * 2, lo + 3 * T * 2)
             s0 = 0
@@ -114,8 +129,8 @@ def tile_moe_shr_lin_gelu_kernel(tc, xT, w, b, gate, offs, pos1, pos2, out):
         xi, xq, xsc = {}, {}, {}
 
         def weave(g, s0, s1):
-            if s0 == 0:
-                xi[g] = ring.tile([P, 4 * S], BF16, name="xi", align_bytes=64)
+            if g not in xi:
+                xi[g] = ring.tile([P, 4 * S], BF16, name="xi", bufs=3, align_bytes=64)
             word = I32 if (g, s0) in WEAVE_V else F32
             dst = xi[g][:, 4 * s0 : 4 * s1].bitcast(word).rearrange("p (s u) -> p s u", u=2)
             src = gw[g][:, :, 2 * s0 : 2 * s1].bitcast(word).rearrange("p u s -> p s u")
@@ -125,7 +140,7 @@ def tile_moe_shr_lin_gelu_kernel(tc, xT, w, b, gate, offs, pos1, pos2, out):
                 nc.scalar.copy(dst, src)
 
         def quant_x(g, s0, s1):
-            if s0 == 0:
+            if g not in xq:
                 xq[g] = keep.tile([P, S], U32, name=f"xq{g}", align_bytes=64)
                 xsc[g] = keep.tile([P, S], U8, name=f"xsc{g}", align_bytes=64)
             nc.vector.quantize_mx(out=xq[g][:, s0:s1].bitcast(FP8X4), scales=xsc[g][:, s0:s1], in_=xi[g][:, 4 * s0 : 4 * s1])
@@ -154,6 +169,8 @@ def tile_moe_shr_lin_gelu_kernel(tc, xT, w, b, gate, offs, pos1, pos2, out):
             if g == 0:
                 ps[e, m] = psum.tile([P, T], F32, name="ps")
             h, i = e // 2, e % 2
+            if e == E:
+                i = QSG[g].index(g)
             n0 = i * N + m * P
             if e < E:
                 o, r, rs = ps[e, m][:, 0:C], xq[g][:, e * C : (e + 1) * C], xsc[g][:, e * C : (e + 1) * C]
@@ -175,13 +192,8 @@ def tile_moe_shr_lin_gelu_kernel(tc, xT, w, b, gate, offs, pos1, pos2, out):
             else:
                 nc.scalar.activation(out=ys[m][:], in_=ps[e, m][:], func=GELU, bias=bias[:, m, e : e + 1])
 
-        a = [keep.tile([P, T], F32, name=f"a{m}") for m in range(M)]
-        bb = [keep.tile([P, T], F32, name=f"bb{m}") for m in range(M)]
-        s = [keep.tile([P, T], F32, name=f"s{m}") for m in range(M)]
-        o = [keep.tile([P, T], F32, name=f"o{m}") for m in range(M)]
-
         def pick(m, r, dst, pos):
-            nc.vector.tensor_tensor(dst[:], y[m][:].indirect(pos[:]), gates[:, r, m, :], MULT)
+            nc.vector.tensor_tensor(dst, y[m][:].indirect(pos[:]), gates[:, r, m, :], MULT)
 
         def load_gates():
             nc.sync.dma_start(pos1_t[:], pos1)
@@ -192,129 +204,103 @@ def tile_moe_shr_lin_gelu_kernel(tc, xT, w, b, gate, offs, pos1, pos2, out):
             pick(m, r, (a, bb)[r][m], (pos1_t, pos2_t)[r])
 
         def ad(m):
-            nc.vector.tensor_tensor(s[m][:], a[m][:], bb[m][:], ADD)
+            nc.vector.tensor_tensor(s[m], a[m], bb[m], ADD)
 
         def ao(m):
-            nc.vector.tensor_tensor(o[m][:], s[m][:], ys[m][:], ADD)
+            nc.vector.tensor_tensor(o[m], s[m], ys[m][:], ADD)
 
         def st(m):
-            nc.sync.dma_start(out=out[m * P : (m + 1) * P, :], in_=o[m][:])
+            nc.sync.dma_start(out=out[m * P : (m + 1) * P, :], in_=o[m])
 
         load_x(0)
         load_x(1)
-        load_w(0, 0)
         load_x(2)
+        load_w(1, 1)
+        load_w(0, 0)
+        load_w(0, 3)
         load_w(0, 1)
         load_x(3)
-        load_w(0, 2)
-        load_x(4)
-        load_w(0, 3)
-        load_x(5)
-        load_w(1, 0)
-        load_w(1, 1)
-        load_w(1, 2)
-        load_w(1, 3)
-        load_w(2, 0)
         load_w(2, 1)
-        load_w(2, 2)
-        load_w(2, 3)
-        load_w(0, 4)
-        load_w(1, 4)
+        load_x(4)
+        load_w(0, 2)
         load_gates()
+        load_w(1, 4)
+        load_w(1, 3)
+        load_w(1, 0)
+        load_x(5)
+        load_w(2, 3)
         load_w(2, 4)
+        load_w(1, 2)
+        load_w(2, 0)
+        load_w(2, 2)
+        load_w(0, 4)
         cast_x(0, "s", 0, T // 2)
         cast_x(0, "v", T // 2, T)
         cast_x(1, "s")
-        gather(0, (384, 384, 256,))
-        gather(1, (512, 512,))
-        cast_w(0, 0)
-        weave_t(0)
         cast_x(2, "s")
-        cast_w(0, 1)
-        cast_x(3, "s")
+        cast_w(1, 1)
+        gather(0, (384, 384, 256,))
+        cast_w(0, 0)
+        gather(1, (512, 512,))
         gather(2, (1024,))
-        weave(0, 0, 1024)
-        gather(3, (1024,))
+        cast_w(0, 3)
+        cast_x(3, "s")
+        cast_w(0, 1)
         cast_w(0, 2)
+        gather(3, (1024,))
+        weave(0, 0, 1024)
+        weave_t(0)
         cast_x(4, "s")
+        weave_t(1)
+        cast_w(1, 4)
+        cast_w(2, 1)
+        quant_t(1)
+        cast_x(5, "s")
+        cast_w(2, 3)
+        weave(1, 0, 1024)
+        quant_w(0, 1)
         quant_x(0, 0, 1024)
         gather(4, (1024,))
-        cast_w(0, 3)
-        cast_x(5, "s")
-        quant_t(0)
-        quant_w(0, 0)
-        weave(1, 0, 1024)
-        gather(5, (512, 512,))
-        quant_w(0, 1)
-        mm(0, 0, 0)
-        mm(0, 0, 1)
-        mm(0, 1, 0)
-        mm(0, 1, 1)
-        mm(0, 2, 0)
-        mm(0, 2, 1)
-        mm(0, 3, 0)
-        mm(0, 3, 1)
-        cast_w(1, 0)
-        cast_w(1, 1)
-        weave(2, 0, 512)
-        weave(2, 512, 1024)
-        cast_w(1, 2)
+        gather(5, (1024,))
         cast_w(1, 3)
-        quant_x(1, 0, 1024)
-        quant_w(1, 0)
-        quant_x(2, 0, 512)
-        quant_x(2, 512, 1024)
-        quant_w(1, 1)
-        mm(1, 0, 0)
-        mm(1, 0, 1)
-        mm(1, 1, 0)
-        mm(1, 1, 1)
-        mm(1, 2, 0)
-        mm(1, 2, 1)
-        mm(1, 3, 0)
-        mm(1, 3, 1)
+        cast_w(1, 0)
+        weave(2, 512, 1024)
         cast_w(2, 0)
-        cast_w(2, 1)
-        quant_w(2, 0)
-        cast_w(2, 2)
-        cast_w(2, 3)
-        quant_w(2, 1)
-        mm(2, 0, 0)
-        mm(2, 1, 0)
-        mm(2, 2, 0)
-        mm(2, 3, 0)
-        mm(2, 0, 1)
-        mm(2, 1, 1)
-        mm(2, 2, 1)
-        mm(2, 3, 1)
-        weave_t(1)
-        quant_t(1)
-        cast_w(0, 4)
-        gelu(0, 0)
-        gelu(1, 0)
-        gelu(2, 0)
-        gelu(3, 0)
-        gelu(0, 1)
-        gelu(1, 1)
-        gelu(2, 1)
-        gelu(3, 1)
+        quant_x(1, 0, 1024)
+        cast_w(1, 2)
+        weave(2, 0, 512)
+        quant_w(0, 0)
+        quant_w(1, 1)
+        quant_w(1, 0)
+        quant_x(2, 0, 1024)
         weave_t(2)
         quant_t(2)
-        quant_w(0, 2)
-        cast_w(1, 4)
-        quant_w(1, 2)
+        cast_w(0, 4)
+        [mm(0, e, m) for e in range(E) for m in range(M)]
+        cast_w(2, 2)
         cast_w(2, 4)
+        quant_w(2, 0)
+        quant_w(2, 1)
+        [mm(1, e, m) for e in range(E) for m in range(M)]
+        [mm(2, e, m) for m in range(M) for e in range(E)]
+        [gelu(e, 0) for e in range(E)]
+        quant_s((0, 1,))
+        [gelu(e, 1) for e in range(E)]
+        quant_t(0)
+        [mm(0, E, m) for m in range(M)]
+        quant_s((2,))
+        [mm(1, E, m) for m in range(M)]
+        [mm(2, E, m) for m in range(M)]
+        [gelu(E, m) for m in range(M)]
+        ab = [ring.tile([P, 2, T], F32, name="wraw", bufs=8) for m in range(M)]
+        so = [ring.tile([P, 2, T], F32, name="wraw", bufs=8) for m in range(M)]
+        a = [ab[m][:, 0, :] for m in range(M)]
+        bb = [ab[m][:, 1, :] for m in range(M)]
+        s = [so[m][:, 0, :] for m in range(M)]
+        o = [so[m][:, 1, :] for m in range(M)]
+
         pk(0, 0)
         pk(0, 1)
-        quant_w(2, 2)
-        mm(0, 4, 0)
-        mm(0, 4, 1)
-        mm(1, 4, 0)
-        mm(1, 4, 1)
-        mm(2, 4, 0)
-        mm(2, 4, 1)
-        gelu(4, 0)
-        gelu(4, 1)
         pk(1, 0)
         ad(0)
         pk(1, 1)

@@ -14,298 +14,268 @@ MULT = mybir.AluOpType.mult
 GELU = mybir.ActivationFunctionType.Gelu_apprx_tanh
 
 P = 128
-K, T, E, C, N = 1536, 512, 4, 256, 256
-S = E * C
-G = K // 512
-M = N // P
-FLOPS = 2 * K * N * (S + T)
+K, T, N = 1536, 512, 256
+E, C = 4, 256
+SHARED = E
+SLOTS = E * C
+J = 4
+K_PASS = P * J
+PASSES = K // K_PASS
+M_TILES = N // P
+LANES = 16
 
-GPS = ()
-WEAVE_V = ((0, 0), (1, 0), (2, 0), (2, 512), )
-WEAVE_T = (1, )
-QSG = {0: (0, 1), 1: (0, 1), 2: (2,)}
+FLOPS = 2 * K * N * (SLOTS + T)
+
+ROUTED = [(g, e) for g in range(PASSES) for e in range(E)]
+CHUNKS = ROUTED + [(g, SHARED) for g in range(PASSES)]
+SHARED_GROUPS = [((0, SHARED), (1, SHARED)), ((2, SHARED),)]
+GROUPS = [tuple(ROUTED[i : i + 2]) for i in range(0, len(ROUTED), 2)] + SHARED_GROUPS
+PLACE = {chunk: (i, slot) for i, group in enumerate(GROUPS) for slot, chunk in enumerate(group)}
 
 
 def tile_moe_shr_lin_gelu_kernel(tc, xT, w, b, gate, offs, pos1, pos2, out):
     nc = tc.nc
-    planes = 2 * G
+
     with ExitStack() as ctx:
         keep = ctx.enter_context(tc.tile_pool(name="keep", bufs=1))
-        ring = ctx.enter_context(tc.tile_pool(name="ring", bufs=2))
+        landing = ctx.enter_context(tc.tile_pool(name="landing", bufs=8))
         psum = ctx.enter_context(tc.psum_pool(name="psum", bufs=8))
 
-        offs_t = keep.tile([P, S // 16], U16, name="offs_t")
-        pos1_t = keep.tile([P, T // 16], U16, name="pos1_t")
-        pos2_t = keep.tile([P, T // 16], U16, name="pos2_t")
-        bias = keep.tile([P, M, E + 1], F32, name="bias")
-        gates = keep.tile([P, 2, M, T], F32, name="gates")
-        xp = keep.tile([P, planes * T * 2], BF16, name="xp", align_bytes=64)
-        y = [keep.tile([P, S], F32, name=f"y{m}") for m in range(M)]
-        ys = [keep.tile([P, T], F32, name=f"ys{m}") for m in range(M)]
+        offsets = keep.tile([P, SLOTS // LANES], U16, name="offsets")
+        positions = [keep.tile([P, T // LANES], U16, name=f"positions{r}") for r in range(2)]
+        bias = keep.tile([P, M_TILES, E + 1], F32, name="bias")
+        gates = [[keep.tile([P, T], F32, name=f"gate{m}{r}") for r in range(2)] for m in range(M_TILES)]
 
-        nc.scalar.dma_start(out=bias[:], in_=b.rearrange("(m p) e -> p m e", p=P))
-        warm = keep.tile([P, 1], F32, name="warm")
-        nc.vector.memset(warm[:], 0.0)
-        warm2 = keep.tile([P, 1], F32, name="warm2")
-        nc.scalar.activation(out=warm2[:], in_=warm[:], func=GELU)
+        pairs = keep.tile([P, 2 * PASSES * T * 2], BF16, name="pairs", align_bytes=64)
+        picked = [keep.tile([P, 2, SLOTS * 2], BF16, name=f"picked{g}", align_bytes=64) for g in range(PASSES)]
+        slot_rows = [keep.tile([P, SLOTS * J], BF16, name=f"slot_rows{g}", align_bytes=64) for g in range(PASSES)]
+        token_rows = [keep.tile([P, T * J], BF16, name=f"token_rows{g}", align_bytes=64) for g in range(PASSES)]
+        w_rows = [keep.tile([P, len(group), N * J], BF16, name=f"w_rows{i}", align_bytes=64) for i, group in enumerate(GROUPS)]
 
-        nc.sync.dma_start(offs_t[:], offs)
-        xraw, wraw = {}, {}
+        slot_codes = [keep.tile([P, SLOTS], U32, name=f"slot_codes{g}", align_bytes=64) for g in range(PASSES)]
+        slot_scales = [keep.tile([P, SLOTS], U8, name=f"slot_scales{g}", align_bytes=64) for g in range(PASSES)]
+        token_codes = [keep.tile([P, T], U32, name=f"token_codes{g}", align_bytes=64) for g in range(PASSES)]
+        token_scales = [keep.tile([P, T], U8, name=f"token_scales{g}", align_bytes=64) for g in range(PASSES)]
+        w_codes = [keep.tile([P, len(group) * N], U32, name=f"w_codes{i}", align_bytes=64) for i, group in enumerate(GROUPS)]
+        w_scales = [keep.tile([P, len(group) * N], U8, name=f"w_scales{i}", align_bytes=64) for i, group in enumerate(GROUPS)]
 
-        def load_x(q):
-            g, u = q // 2, 1 - q % 2
-            xraw[q] = keep.tile([P, 2, T], F32, name=f"xraw{q}")
-            rows = xT[g * 512 : (g + 1) * 512, :].rearrange("(p u e) t -> u p e t", u=2, e=2)
-            if q == 0:
-                for t0 in (0, T // 2):
-                    nc.sync.dma_start(out=xraw[q][:, :, t0 : t0 + T // 2], in_=rows[u][:, :, t0 : t0 + T // 2])
-            else:
-                nc.sync.dma_start(out=xraw[q][:], in_=rows[u])
+        slot_results = [keep.tile([P, SLOTS], F32, name=f"slot_results{m}") for m in range(M_TILES)]
+        shared_results = [keep.tile([P, T], F32, name=f"shared_results{m}") for m in range(M_TILES)]
+
+        x_raw = {0: keep.tile([P, 2, 2, T], F32, name="x_raw0")}
+        for g in range(1, PASSES):
+            x_raw[g] = keep.tile([P, J, T], F32, name=f"x_raw{g}")
+        w_raw = {}
+        banks = {}
+
+        zero = keep.tile([P, 1], F32, name="zero")
+        unused = keep.tile([P, 1], F32, name="unused")
+        nc.vector.memset(zero[:], 0.0)
+        nc.scalar.activation(out=unused[:], in_=zero[:], func=GELU)
+
+
+        def rows_of_pass(g):
+            return slice(g * K_PASS, (g + 1) * K_PASS)
+
+        def load_x_pair(h, tokens):
+            source = xT[rows_of_pass(0), :].rearrange("(p h i) t -> h p i t", h=2, i=2)
+            nc.sync.dma_start(out=x_raw[0][:, h, :, tokens], in_=source[h][:, :, tokens])
+
+        def load_x_pass(g):
+            nc.sync.dma_start(out=x_raw[g][:], in_=xT[rows_of_pass(g), :].rearrange("(p j) t -> p j t", j=J))
 
         def load_w(g, e):
-            wraw[g, e] = ring.tile([P, 4, N], F32, name="wraw", bufs=8)
-            nc.sync.dma_start(out=wraw[g, e][:], in_=w[e, g * 512 : (g + 1) * 512, :].rearrange("(p j) n -> p j n", j=4))
+            w_raw[g, e] = landing.tile([P, J, N], F32, name="w_raw")
+            nc.sync.dma_start(out=w_raw[g, e][:], in_=w[e, rows_of_pass(g), :].rearrange("(p j) n -> p j n", j=J))
 
-        def cast_x(q, engine, t0=0, t1=T):
-            base = (planes - 1 - q) * T * 2
-            dst = xp[:, base + 2 * t0 : base + 2 * t1].rearrange("p (t e) -> p t e", e=2)
-            src = xraw[q][:, :, t0:t1].rearrange("p e t -> p t e")
-            if engine == "v":
-                nc.vector.tensor_copy(dst, src)
-            else:
-                nc.scalar.copy(dst, src)
 
-        wb = {}
+        def plane_start(g, h):
+            return (2 * (PASSES - 1 - g) + h) * T * 2
+
+        def cast_x_pair(copy, h, tokens):
+            start = plane_start(0, h)
+            plane = pairs[:, start : start + 2 * T].rearrange("p (t i) -> p t i", i=2)
+            copy(plane[:, tokens, :], x_raw[0][:, h, :, tokens].rearrange("p i t -> p t i"))
+
+        def cast_x_pass(g):
+            start = plane_start(g, 0)
+            planes = pairs[:, start : start + 4 * T].rearrange("p (h t i) -> p h t i", h=2, i=2)
+            nc.scalar.copy(planes, x_raw[g][:].rearrange("p (h i) t -> p h t i", i=2))
+
+        def gather(g, h, pieces):
+            start = plane_start(g, h)
+            window = pairs[:, start : min(start + 3 * 2 * T, 2 * PASSES * 2 * T)].bitcast(U32)
+            first = 0
+            for count in pieces:
+                nc.vector.tensor_copy(
+                    picked[g][:, h, 2 * first : 2 * (first + count)].bitcast(U32),
+                    window.indirect(offsets[:, first // LANES : (first + count) // LANES]),
+                )
+                first += count
+
+        def join_slot_pairs(g, slots):
+            words = slice(2 * slots.start, 2 * slots.stop)
+            rows = slot_rows[g][:, J * slots.start : J * slots.stop].bitcast(I32).rearrange("p (s h) -> p s h", h=2)
+            nc.vector.tensor_copy(rows, picked[g][:, :, words].bitcast(I32).rearrange("p h s -> p s h"))
+
+        def join_token_pairs(copy, word, g):
+            start = plane_start(g, 0)
+            planes = pairs[:, start : start + 4 * T].bitcast(word).rearrange("p (h t) -> p t h", h=2)
+            copy(token_rows[g][:].bitcast(word).rearrange("p (t h) -> p t h", h=2), planes)
+
+        def quantize(codes, scales, rows):
+            nc.vector.quantize_mx(out=codes[:].bitcast(FP8X4), scales=scales[:], in_=rows)
+
+        def quantize_slots(g):
+            quantize(slot_codes[g], slot_scales[g], slot_rows[g][:])
+
+        def quantize_tokens(g):
+            quantize(token_codes[g], token_scales[g], token_rows[g][:])
+
 
         def cast_w(g, e):
-            h, i = e // 2, e % 2
-            if e == E:
-                if (E, QSG[g]) not in wb:
-                    wb[E, QSG[g]] = keep.tile([P, 2, N * 4], BF16, name=f"wbs{g}", align_bytes=64)
-                wb[g, h] = wb[E, QSG[g]]
-                i = QSG[g].index(g)
-            elif (g, h) not in wb:
-                wb[g, h] = ring.tile([P, 2, N * 4], BF16, name="wb", bufs=6, align_bytes=64)
-            dst = wb[g, h][:, i, :].rearrange("p (c i j) -> p c j i", i=4, j=4)
-            srcv = wraw[g, e][:].rearrange("p j (c i) -> p c j i", i=4)
-            if (g, e) in GPS:
-                nc.gpsimd.tensor_scalar(dst, srcv, 1.0, 0.0, MULT, ADD)
-            else:
-                nc.scalar.copy(dst, srcv)
+            i, slot = PLACE[g, e]
+            rows = w_rows[i][:, slot, :].rearrange("p (q c j) -> p q j c", c=4, j=J)
+            nc.scalar.copy(rows, w_raw[g, e][:].rearrange("p j (q c) -> p q j c", c=4))
 
-        wq, wsc = {}, {}
+        def quantize_w(i):
+            quantize(w_codes[i], w_scales[i], w_rows[i][:].rearrange("p slot c -> p (slot c)"))
 
-        def quant_w(g, h):
-            n = 2 * N if h < 2 else N
-            wq[g, h] = keep.tile([P, n], U32, name=f"wq{g}{h}", align_bytes=64)
-            wsc[g, h] = keep.tile([P, n], U8, name=f"wsc{g}{h}", align_bytes=64)
-            nc.vector.quantize_mx(out=wq[g, h][:].bitcast(FP8X4), scales=wsc[g, h][:], in_=wb[g, h][:].rearrange("p i n -> p (i n)")[:, 0 : 4 * n])
 
-        def quant_s(gs):
-            n = len(gs) * N
-            codes = keep.tile([P, n], U32, name=f"wqs{gs[0]}", align_bytes=64)
-            scales = keep.tile([P, n], U8, name=f"wscs{gs[0]}", align_bytes=64)
-            nc.vector.quantize_mx(out=codes[:].bitcast(FP8X4), scales=scales[:], in_=wb[E, gs][:].rearrange("p i n -> p (i n)")[:, 0 : 4 * n])
-            for i, g in enumerate(gs):
-                wq[g, 2] = codes
-                wsc[g, 2] = scales
-
-        gw = {}
-
-        def gather(q, cuts):
-            g, u = q // 2, 1 - q % 2
-            if g not in gw:
-                gw[g] = ring.tile([P, 2, 2 * S], BF16, name="gw", bufs=3, align_bytes=64)
-            lo = (planes - 1 - q) * T * 2
-            hi = min(planes * T * 2, lo + 3 * T * 2)
-            s0 = 0
-            for n in cuts:
-                nc.vector.tensor_copy(
-                    gw[g][:, u, 2 * s0 : 2 * (s0 + n)].bitcast(U32),
-                    xp[:, lo:hi].bitcast(U32).indirect(offs_t[:, s0 // 16 : (s0 + n) // 16]),
-                )
-                s0 += n
-
-        xi, xq, xsc = {}, {}, {}
-
-        def weave(g, s0, s1):
-            if g not in xi:
-                xi[g] = ring.tile([P, 4 * S], BF16, name="xi", bufs=3, align_bytes=64)
-            word = I32 if (g, s0) in WEAVE_V else F32
-            dst = xi[g][:, 4 * s0 : 4 * s1].bitcast(word).rearrange("p (s u) -> p s u", u=2)
-            src = gw[g][:, :, 2 * s0 : 2 * s1].bitcast(word).rearrange("p u s -> p s u")
-            if (g, s0) in WEAVE_V:
-                nc.vector.tensor_copy(dst, src)
-            else:
-                nc.scalar.copy(dst, src)
-
-        def quant_x(g, s0, s1):
-            if g not in xq:
-                xq[g] = keep.tile([P, S], U32, name=f"xq{g}", align_bytes=64)
-                xsc[g] = keep.tile([P, S], U8, name=f"xsc{g}", align_bytes=64)
-            nc.vector.quantize_mx(out=xq[g][:, s0:s1].bitcast(FP8X4), scales=xsc[g][:, s0:s1], in_=xi[g][:, 4 * s0 : 4 * s1])
-
-        ti, tq, tsc = {}, {}, {}
-
-        def weave_t(g):
-            ti[g] = ring.tile([P, 4 * T], BF16, name="ti", bufs=3, align_bytes=64)
-            base = (planes - 2 - 2 * g) * T * 2
-            word = I32 if g in WEAVE_T else F32
-            two = xp[:, base : base + 4 * T].bitcast(word).rearrange("p (u t) -> p t u", u=2)
-            dst = ti[g][:].bitcast(word).rearrange("p (t u) -> p t u", u=2)
-            if g in WEAVE_T:
-                nc.vector.tensor_copy(dst, two)
-            else:
-                nc.scalar.copy(dst, two)
-
-        def quant_t(g):
-            tq[g] = keep.tile([P, T], U32, name=f"tq{g}", align_bytes=64)
-            tsc[g] = keep.tile([P, T], U8, name=f"tsc{g}", align_bytes=64)
-            nc.vector.quantize_mx(out=tq[g][:].bitcast(FP8X4), scales=tsc[g][:], in_=ti[g][:])
-
-        ps = {}
-
-        def mm(g, e, m):
+        def multiply(g, e, m):
             if g == 0:
-                ps[e, m] = psum.tile([P, T], F32, name="ps")
-            h, i = e // 2, e % 2
-            if e == E:
-                i = QSG[g].index(g)
-            n0 = i * N + m * P
-            if e < E:
-                o, r, rs = ps[e, m][:, 0:C], xq[g][:, e * C : (e + 1) * C], xsc[g][:, e * C : (e + 1) * C]
+                banks[e, m] = psum.tile([P, T], F32, name="bank")
+            i, slot = PLACE[g, e]
+            channels = slice(slot * N + m * P, slot * N + (m + 1) * P)
+            if e == SHARED:
+                codes, scales, columns = token_codes[g], token_scales[g], slice(0, T)
             else:
-                o, r, rs = ps[e, m][:], tq[g][:], tsc[g][:]
+                codes, scales, columns = slot_codes[g], slot_scales[g], slice(e * C, (e + 1) * C)
             nc.tensor.matmul_mx(
-                out=o,
-                lhsT=wq[g, h][:, n0 : n0 + P].bitcast(FP8X4),
-                lhsT_scale=wsc[g, h][:, n0 : n0 + P],
-                rhs=r.bitcast(FP8X4),
-                rhs_scale=rs,
+                out=banks[e, m][:, 0 : columns.stop - columns.start],
+                lhsT=w_codes[i][:, channels].bitcast(FP8X4),
+                lhsT_scale=w_scales[i][:, channels],
+                rhs=codes[:, columns].bitcast(FP8X4),
+                rhs_scale=scales[:, columns],
                 start=(g == 0),
-                stop=(g == G - 1),
+                stop=(g == PASSES - 1),
             )
 
-        def gelu(e, m):
-            if e < E:
-                nc.scalar.activation(out=y[m][:, e * C : (e + 1) * C], in_=ps[e, m][:, 0:C], func=GELU, bias=bias[:, m, e : e + 1])
+        def activate(e, m):
+            if e == SHARED:
+                result, columns = shared_results[m][:], T
             else:
-                nc.scalar.activation(out=ys[m][:], in_=ps[e, m][:], func=GELU, bias=bias[:, m, e : e + 1])
+                result, columns = slot_results[m][:, e * C : (e + 1) * C], C
+            nc.scalar.activation(out=result, in_=banks[e, m][:, 0:columns], func=GELU, bias=bias[:, m, e : e + 1])
 
-        def pick(m, r, dst, pos):
-            nc.vector.tensor_tensor(dst, y[m][:].indirect(pos[:]), gates[:, r, m, :], MULT)
 
-        def load_gates():
-            nc.sync.dma_start(pos1_t[:], pos1)
-            nc.sync.dma_start(pos2_t[:], pos2)
-            nc.sync.dma_start(out=gates[:], in_=gate.rearrange("r (m p) t -> p r m t", p=P))
+        halves = (slice(0, T // 2), slice(T // 2, T))
+        whole = slice(0, T)
+        for tokens in halves:
+            load_x_pair(1, tokens)
+        nc.sync.dma_start(offsets[:], offs)
+        load_x_pair(0, whole)
+        load_x_pass(1)
+        for chunk in CHUNKS[:6]:
+            load_w(*chunk)
+        load_x_pass(2)
+        for chunk in CHUNKS[6:]:
+            load_w(*chunk)
+        nc.sync.dma_start(out=bias[:], in_=b.rearrange("(m p) e -> p m e", p=P))
+        nc.sync.dma_start(positions[0][:], pos1)
+        nc.sync.dma_start(positions[1][:], pos2)
+        for m in range(M_TILES):
+            for r in range(2):
+                nc.sync.dma_start(out=gates[m][r][:], in_=gate[r, m * P : (m + 1) * P, :])
 
-        def pk(m, r):
-            pick(m, r, (a, bb)[r][m], (pos1_t, pos2_t)[r])
+        cast_x_pair(nc.scalar.copy, 1, halves[0])
+        cast_x_pair(nc.vector.tensor_copy, 1, halves[1])
+        gather(0, 1, (384, 384, 256))
+        cast_x_pair(nc.scalar.copy, 0, whole)
+        gather(0, 0, (512, 512))
+        join_token_pairs(nc.scalar.copy, F32, 0)
+        quantize_tokens(0)
+        join_slot_pairs(0, slice(0, SLOTS))
+        cast_x_pass(1)
+        gather(1, 1, (SLOTS,))
+        quantize_slots(0)
+        gather(1, 0, (SLOTS,))
+        join_token_pairs(nc.vector.tensor_copy, I32, 1)
+        join_slot_pairs(1, slice(0, SLOTS))
 
-        def ad(m):
-            nc.vector.tensor_tensor(s[m], a[m], bb[m], ADD)
+        for chunk in CHUNKS[0:2]:
+            cast_w(*chunk)
+        quantize_w(0)
+        quantize_tokens(1)
+        quantize_slots(1)
+        for chunk in CHUNKS[2:6]:
+            cast_w(*chunk)
+        cast_x_pass(2)
+        gather(2, 1, (SLOTS,))
+        quantize_w(1)
+        for e in range(E):
+            for m in range(M_TILES):
+                multiply(0, e, m)
+        gather(2, 0, (SLOTS,))
+        quantize_w(2)
+        join_slot_pairs(2, slice(0, SLOTS // 2))
+        join_slot_pairs(2, slice(SLOTS // 2, SLOTS))
+        for chunk in CHUNKS[6:8]:
+            cast_w(*chunk)
+        quantize_w(3)
+        for e in range(E):
+            for m in range(M_TILES):
+                multiply(1, e, m)
+        quantize_slots(2)
 
-        def ao(m):
-            nc.vector.tensor_tensor(o[m], s[m], ys[m][:], ADD)
+        for chunk in CHUNKS[8:12]:
+            cast_w(*chunk)
+        join_token_pairs(nc.scalar.copy, F32, 2)
+        quantize_tokens(2)
+        quantize_w(4)
+        quantize_w(5)
+        for m in range(M_TILES):
+            for e in range(E):
+                multiply(2, e, m)
 
-        def st(m):
-            nc.sync.dma_start(out=out[m * P : (m + 1) * P, :], in_=o[m])
+        for chunk in CHUNKS[12:]:
+            cast_w(*chunk)
+        quantize_w(6)
+        quantize_w(7)
+        for m in range(M_TILES):
+            for e in range(E):
+                activate(e, m)
+        for g in range(PASSES):
+            for m in range(M_TILES):
+                multiply(g, SHARED, m)
+        for m in range(M_TILES):
+            activate(SHARED, m)
 
-        load_x(0)
-        load_x(1)
-        load_x(2)
-        load_w(1, 1)
-        load_w(0, 0)
-        load_w(0, 3)
-        load_w(0, 1)
-        load_x(3)
-        load_w(2, 1)
-        load_x(4)
-        load_w(0, 2)
-        load_gates()
-        load_w(1, 4)
-        load_w(1, 3)
-        load_w(1, 0)
-        load_x(5)
-        load_w(2, 3)
-        load_w(2, 4)
-        load_w(1, 2)
-        load_w(2, 0)
-        load_w(2, 2)
-        load_w(0, 4)
-        cast_x(0, "s", 0, T // 2)
-        cast_x(0, "v", T // 2, T)
-        cast_x(1, "s")
-        cast_x(2, "s")
-        cast_w(1, 1)
-        gather(0, (384, 384, 256,))
-        cast_w(0, 0)
-        gather(1, (512, 512,))
-        gather(2, (1024,))
-        cast_w(0, 3)
-        cast_x(3, "s")
-        cast_w(0, 1)
-        cast_w(0, 2)
-        gather(3, (1024,))
-        weave(0, 0, 1024)
-        weave_t(0)
-        cast_x(4, "s")
-        weave_t(1)
-        cast_w(1, 4)
-        cast_w(2, 1)
-        quant_t(1)
-        cast_x(5, "s")
-        cast_w(2, 3)
-        weave(1, 0, 1024)
-        quant_w(0, 1)
-        quant_x(0, 0, 1024)
-        gather(4, (1024,))
-        gather(5, (1024,))
-        cast_w(1, 3)
-        cast_w(1, 0)
-        weave(2, 512, 1024)
-        cast_w(2, 0)
-        quant_x(1, 0, 1024)
-        cast_w(1, 2)
-        weave(2, 0, 512)
-        quant_w(0, 0)
-        quant_w(1, 1)
-        quant_w(1, 0)
-        quant_x(2, 0, 1024)
-        weave_t(2)
-        quant_t(2)
-        cast_w(0, 4)
-        [mm(0, e, m) for e in range(E) for m in range(M)]
-        cast_w(2, 2)
-        cast_w(2, 4)
-        quant_w(2, 0)
-        quant_w(2, 1)
-        [mm(1, e, m) for e in range(E) for m in range(M)]
-        [mm(2, e, m) for m in range(M) for e in range(E)]
-        [gelu(e, 0) for e in range(E)]
-        quant_s((0, 1,))
-        [gelu(e, 1) for e in range(E)]
-        quant_t(0)
-        [mm(0, E, m) for m in range(M)]
-        quant_s((2,))
-        [mm(1, E, m) for m in range(M)]
-        [mm(2, E, m) for m in range(M)]
-        [gelu(E, m) for m in range(M)]
-        ab = [ring.tile([P, 2, T], F32, name="wraw", bufs=8) for m in range(M)]
-        so = [ring.tile([P, 2, T], F32, name="wraw", bufs=8) for m in range(M)]
-        a = [ab[m][:, 0, :] for m in range(M)]
-        bb = [ab[m][:, 1, :] for m in range(M)]
-        s = [so[m][:, 0, :] for m in range(M)]
-        o = [so[m][:, 1, :] for m in range(M)]
+        products = [landing.tile([P, 2, T], F32, name="w_raw") for m in range(M_TILES)]
+        sums = [landing.tile([P, 2, T], F32, name="w_raw") for m in range(M_TILES)]
 
-        pk(0, 0)
-        pk(0, 1)
-        pk(1, 0)
-        ad(0)
-        pk(1, 1)
-        ao(0)
-        st(0)
-        ad(1)
-        ao(1)
-        st(1)
+        def fetch(m, r):
+            picked_slots = slot_results[m][:].indirect(positions[r][:])
+            nc.vector.tensor_tensor(products[m][:, r, :], picked_slots, gates[m][r][:], MULT)
+
+        def add_products(m):
+            nc.vector.tensor_tensor(sums[m][:, 0, :], products[m][:, 0, :], products[m][:, 1, :], ADD)
+
+        def add_shared(m, parts):
+            for tokens in parts:
+                nc.vector.tensor_tensor(sums[m][:, 1, tokens], sums[m][:, 0, tokens], shared_results[m][:, tokens], ADD)
+
+        def store(m, parts):
+            for tokens in parts:
+                nc.sync.dma_start(out=out[m * P : (m + 1) * P, tokens], in_=sums[m][:, 1, tokens])
+
+        fetch(0, 0)
+        fetch(0, 1)
+        fetch(1, 0)
+        add_products(0)
+        fetch(1, 1)
+        add_shared(0, (whole,))
+        store(0, (whole,))
+        add_products(1)
+        add_shared(1, halves)
+        store(1, halves)

from contextlib import ExitStack

import concourse.mybir as mybir

F32 = mybir.dt.float32
BF16 = mybir.dt.bfloat16
I32 = mybir.dt.int32
U32 = mybir.dt.uint32
U16 = mybir.dt.uint16
U8 = mybir.dt.uint8
FP8X4 = mybir.dt.float8_e4m3fn_x4
ADD = mybir.AluOpType.add
MULT = mybir.AluOpType.mult
GELU = mybir.ActivationFunctionType.Gelu_apprx_tanh

P = 128
K, T, N = 1536, 512, 256
E, C = 4, 256
SHARED = E
SLOTS = E * C
J = 4
K_PASS = P * J
PASSES = K // K_PASS
M_TILES = N // P
LANES = 16

FLOPS = 2 * K * N * (SLOTS + T)

ROUTED = [(g, e) for g in range(PASSES) for e in range(E)]
CHUNKS = ROUTED + [(g, SHARED) for g in range(PASSES)]
SHARED_GROUPS = [((0, SHARED), (1, SHARED)), ((2, SHARED),)]
GROUPS = [tuple(ROUTED[i : i + 2]) for i in range(0, len(ROUTED), 2)] + SHARED_GROUPS
PLACE = {chunk: (i, slot) for i, group in enumerate(GROUPS) for slot, chunk in enumerate(group)}


def tile_moe_shr_lin_gelu_kernel(tc, xT, w, b, gate, offs, pos1, pos2, out):
    nc = tc.nc

    with ExitStack() as ctx:
        keep = ctx.enter_context(tc.tile_pool(name="keep", bufs=1))
        landing = ctx.enter_context(tc.tile_pool(name="landing", bufs=8))
        psum = ctx.enter_context(tc.psum_pool(name="psum", bufs=8))

        offsets = keep.tile([P, SLOTS // LANES], U16, name="offsets")
        positions = [keep.tile([P, T // LANES], U16, name=f"positions{r}") for r in range(2)]
        bias = keep.tile([P, M_TILES, E + 1], F32, name="bias")
        gates = [[keep.tile([P, T], F32, name=f"gate{m}{r}") for r in range(2)] for m in range(M_TILES)]

        pairs = keep.tile([P, 2 * PASSES * T * 2], BF16, name="pairs", align_bytes=64)
        picked = [keep.tile([P, 2, SLOTS * 2], BF16, name=f"picked{g}", align_bytes=64) for g in range(PASSES)]
        slot_rows = [keep.tile([P, SLOTS * J], BF16, name=f"slot_rows{g}", align_bytes=64) for g in range(PASSES)]
        token_rows = [keep.tile([P, T * J], BF16, name=f"token_rows{g}", align_bytes=64) for g in range(PASSES)]
        w_rows = [keep.tile([P, len(group), N * J], BF16, name=f"w_rows{i}", align_bytes=64) for i, group in enumerate(GROUPS)]

        slot_codes = [keep.tile([P, SLOTS], U32, name=f"slot_codes{g}", align_bytes=64) for g in range(PASSES)]
        slot_scales = [keep.tile([P, SLOTS], U8, name=f"slot_scales{g}", align_bytes=64) for g in range(PASSES)]
        token_codes = [keep.tile([P, T], U32, name=f"token_codes{g}", align_bytes=64) for g in range(PASSES)]
        token_scales = [keep.tile([P, T], U8, name=f"token_scales{g}", align_bytes=64) for g in range(PASSES)]
        w_codes = [keep.tile([P, len(group) * N], U32, name=f"w_codes{i}", align_bytes=64) for i, group in enumerate(GROUPS)]
        w_scales = [keep.tile([P, len(group) * N], U8, name=f"w_scales{i}", align_bytes=64) for i, group in enumerate(GROUPS)]

        slot_results = [keep.tile([P, SLOTS], F32, name=f"slot_results{m}") for m in range(M_TILES)]
        shared_results = [keep.tile([P, T], F32, name=f"shared_results{m}") for m in range(M_TILES)]

        x_raw = {0: keep.tile([P, 2, 2, T], F32, name="x_raw0")}
        for g in range(1, PASSES):
            x_raw[g] = keep.tile([P, J, T], F32, name=f"x_raw{g}")
        w_raw = {}
        banks = {}

        zero = keep.tile([P, 1], F32, name="zero")
        unused = keep.tile([P, 1], F32, name="unused")
        nc.vector.memset(zero[:], 0.0)
        nc.scalar.activation(out=unused[:], in_=zero[:], func=GELU)


        def rows_of_pass(g):
            return slice(g * K_PASS, (g + 1) * K_PASS)

        def load_x_pair(h, tokens):
            source = xT[rows_of_pass(0), :].rearrange("(p h i) t -> h p i t", h=2, i=2)
            nc.sync.dma_start(out=x_raw[0][:, h, :, tokens], in_=source[h][:, :, tokens])

        def load_x_pass(g):
            nc.sync.dma_start(out=x_raw[g][:], in_=xT[rows_of_pass(g), :].rearrange("(p j) t -> p j t", j=J))

        def load_w(g, e):
            w_raw[g, e] = landing.tile([P, J, N], F32, name="w_raw")
            nc.sync.dma_start(out=w_raw[g, e][:], in_=w[e, rows_of_pass(g), :].rearrange("(p j) n -> p j n", j=J))


        def plane_start(g, h):
            return (2 * (PASSES - 1 - g) + h) * T * 2

        def cast_x_pair(copy, h, tokens):
            start = plane_start(0, h)
            plane = pairs[:, start : start + 2 * T].rearrange("p (t i) -> p t i", i=2)
            copy(plane[:, tokens, :], x_raw[0][:, h, :, tokens].rearrange("p i t -> p t i"))

        def cast_x_pass(g):
            start = plane_start(g, 0)
            planes = pairs[:, start : start + 4 * T].rearrange("p (h t i) -> p h t i", h=2, i=2)
            nc.scalar.copy(planes, x_raw[g][:].rearrange("p (h i) t -> p h t i", i=2))

        def gather(g, h, pieces):
            start = plane_start(g, h)
            window = pairs[:, start : min(start + 3 * 2 * T, 2 * PASSES * 2 * T)].bitcast(U32)
            first = 0
            for count in pieces:
                nc.vector.tensor_copy(
                    picked[g][:, h, 2 * first : 2 * (first + count)].bitcast(U32),
                    window.indirect(offsets[:, first // LANES : (first + count) // LANES]),
                )
                first += count

        def join_slot_pairs(g, slots):
            words = slice(2 * slots.start, 2 * slots.stop)
            rows = slot_rows[g][:, J * slots.start : J * slots.stop].bitcast(I32).rearrange("p (s h) -> p s h", h=2)
            nc.vector.tensor_copy(rows, picked[g][:, :, words].bitcast(I32).rearrange("p h s -> p s h"))

        def join_token_pairs(copy, word, g):
            start = plane_start(g, 0)
            planes = pairs[:, start : start + 4 * T].bitcast(word).rearrange("p (h t) -> p t h", h=2)
            copy(token_rows[g][:].bitcast(word).rearrange("p (t h) -> p t h", h=2), planes)

        def quantize(codes, scales, rows):
            nc.vector.quantize_mx(out=codes[:].bitcast(FP8X4), scales=scales[:], in_=rows)

        def quantize_slots(g):
            quantize(slot_codes[g], slot_scales[g], slot_rows[g][:])

        def quantize_tokens(g):
            quantize(token_codes[g], token_scales[g], token_rows[g][:])


        def cast_w(g, e):
            i, slot = PLACE[g, e]
            rows = w_rows[i][:, slot, :].rearrange("p (q c j) -> p q j c", c=4, j=J)
            nc.scalar.copy(rows, w_raw[g, e][:].rearrange("p j (q c) -> p q j c", c=4))

        def quantize_w(i):
            quantize(w_codes[i], w_scales[i], w_rows[i][:].rearrange("p slot c -> p (slot c)"))


        def multiply(g, e, m):
            if g == 0:
                banks[e, m] = psum.tile([P, T], F32, name="bank")
            i, slot = PLACE[g, e]
            channels = slice(slot * N + m * P, slot * N + (m + 1) * P)
            if e == SHARED:
                codes, scales, columns = token_codes[g], token_scales[g], slice(0, T)
            else:
                codes, scales, columns = slot_codes[g], slot_scales[g], slice(e * C, (e + 1) * C)
            nc.tensor.matmul_mx(
                out=banks[e, m][:, 0 : columns.stop - columns.start],
                lhsT=w_codes[i][:, channels].bitcast(FP8X4),
                lhsT_scale=w_scales[i][:, channels],
                rhs=codes[:, columns].bitcast(FP8X4),
                rhs_scale=scales[:, columns],
                start=(g == 0),
                stop=(g == PASSES - 1),
            )

        def activate(e, m):
            if e == SHARED:
                result, columns = shared_results[m][:], T
            else:
                result, columns = slot_results[m][:, e * C : (e + 1) * C], C
            nc.scalar.activation(out=result, in_=banks[e, m][:, 0:columns], func=GELU, bias=bias[:, m, e : e + 1])


        halves = (slice(0, T // 2), slice(T // 2, T))
        whole = slice(0, T)
        for tokens in halves:
            load_x_pair(1, tokens)
        nc.sync.dma_start(offsets[:], offs)
        load_x_pair(0, whole)
        load_x_pass(1)
        for chunk in CHUNKS[:6]:
            load_w(*chunk)
        load_x_pass(2)
        for chunk in CHUNKS[6:]:
            load_w(*chunk)
        nc.sync.dma_start(out=bias[:], in_=b.rearrange("(m p) e -> p m e", p=P))
        nc.sync.dma_start(positions[0][:], pos1)
        nc.sync.dma_start(positions[1][:], pos2)
        for m in range(M_TILES):
            for r in range(2):
                nc.sync.dma_start(out=gates[m][r][:], in_=gate[r, m * P : (m + 1) * P, :])

        cast_x_pair(nc.scalar.copy, 1, halves[0])
        cast_x_pair(nc.vector.tensor_copy, 1, halves[1])
        gather(0, 1, (384, 384, 256))
        cast_x_pair(nc.scalar.copy, 0, whole)
        gather(0, 0, (512, 512))
        join_token_pairs(nc.scalar.copy, F32, 0)
        quantize_tokens(0)
        join_slot_pairs(0, slice(0, SLOTS))
        cast_x_pass(1)
        gather(1, 1, (SLOTS,))
        quantize_slots(0)
        gather(1, 0, (SLOTS,))
        join_token_pairs(nc.vector.tensor_copy, I32, 1)
        join_slot_pairs(1, slice(0, SLOTS))

        for chunk in CHUNKS[0:2]:
            cast_w(*chunk)
        quantize_w(0)
        quantize_tokens(1)
        quantize_slots(1)
        for chunk in CHUNKS[2:6]:
            cast_w(*chunk)
        cast_x_pass(2)
        gather(2, 1, (SLOTS,))
        quantize_w(1)
        for e in range(E):
            for m in range(M_TILES):
                multiply(0, e, m)
        gather(2, 0, (SLOTS,))
        quantize_w(2)
        join_slot_pairs(2, slice(0, SLOTS // 2))
        join_slot_pairs(2, slice(SLOTS // 2, SLOTS))
        for chunk in CHUNKS[6:8]:
            cast_w(*chunk)
        quantize_w(3)
        for e in range(E):
            for m in range(M_TILES):
                multiply(1, e, m)
        quantize_slots(2)

        for chunk in CHUNKS[8:12]:
            cast_w(*chunk)
        join_token_pairs(nc.scalar.copy, F32, 2)
        quantize_tokens(2)
        quantize_w(4)
        quantize_w(5)
        for m in range(M_TILES):
            for e in range(E):
                multiply(2, e, m)

        for chunk in CHUNKS[12:]:
            cast_w(*chunk)
        quantize_w(6)
        quantize_w(7)
        for m in range(M_TILES):
            for e in range(E):
                activate(e, m)
        for g in range(PASSES):
            for m in range(M_TILES):
                multiply(g, SHARED, m)
        for m in range(M_TILES):
            activate(SHARED, m)

        products = [landing.tile([P, 2, T], F32, name="w_raw") for m in range(M_TILES)]
        sums = [landing.tile([P, 2, T], F32, name="w_raw") for m in range(M_TILES)]

        def fetch(m, r):
            picked_slots = slot_results[m][:].indirect(positions[r][:])
            nc.vector.tensor_tensor(products[m][:, r, :], picked_slots, gates[m][r][:], MULT)

        def add_products(m):
            nc.vector.tensor_tensor(sums[m][:, 0, :], products[m][:, 0, :], products[m][:, 1, :], ADD)

        def add_shared(m, parts):
            for tokens in parts:
                nc.vector.tensor_tensor(sums[m][:, 1, tokens], sums[m][:, 0, tokens], shared_results[m][:, tokens], ADD)

        def store(m, parts):
            for tokens in parts:
                nc.sync.dma_start(out=out[m * P : (m + 1) * P, tokens], in_=sums[m][:, 1, tokens])

        fetch(0, 0)
        fetch(0, 1)
        fetch(1, 0)
        add_products(0)
        fetch(1, 1)
        add_shared(0, (whole,))
        store(0, (whole,))
        add_products(1)
        add_shared(1, halves)
        store(1, halves)
